import numpy as np
import ml_dtypes


def mxq(x, axis, fmt="e4m3"):
    dtype, down = {"e4m3": (ml_dtypes.float8_e4m3fn, 7), "e5m2": (ml_dtypes.float8_e5m2, 14)}[fmt]
    v = np.moveaxis(np.asarray(x, np.float32).astype(ml_dtypes.bfloat16).astype(np.float64), axis, -1)
    blocks = v.reshape(v.shape[:-1] + (-1, 32))
    amax = np.abs(blocks).max(-1, keepdims=True)
    byte = np.maximum(np.where(amax > 0, np.frexp(amax)[1] - 1 + 127, 0) - down, 1)
    scale = np.exp2(byte - 127.0)
    codes = (blocks / scale).astype(np.float32).astype(dtype).astype(np.float64)
    return np.moveaxis((codes * scale).reshape(v.shape), -1, axis)


WIDE = False


def mx_kscale(k):
    if not WIDE:
        return np.ones(k)
    levels = np.array([30, -30])
    if k % 512:
        return np.exp2(np.random.permutation(np.resize(levels, k // 32))).repeat(32)
    a = np.empty((k // 512, 16))
    for p in range(k // 512):
        a[p, :8] = np.random.permutation(np.resize(levels, 8))
        for g in range(8):
            far = levels[np.abs(levels - a[p, g]) >= 10]
            a[p, g + 8] = far[np.random.randint(len(far))]
    return np.exp2(a.ravel()).repeat(32)


def f64(x):
    return np.asarray(x).astype(np.float64)


def striped(idx):
    return np.tile(np.asarray(idx).reshape(-1, 16).T, (8, 1)).astype(np.uint16)


def unstriped(offs):
    return offs[:16].T.reshape(-1).astype(np.int64)


E2M1 = np.array([0.0, 0.5, 1.0, 1.5, 2.0, 3.0, 4.0, 6.0, -0.0, -0.5, -1.0, -1.5, -2.0, -3.0, -4.0, -6.0])


def pack_weight(w, fmt):
    k, n = w.shape
    w = f64(np.asarray(w, np.float32).astype(ml_dtypes.bfloat16)).reshape(k // 32, 32, n)
    amax = np.abs(w).max(1)
    if fmt in ("e4m3", "e5m2"):
        byte = np.frexp(amax)[1] - 1 + 127 - (7 if fmt == "e4m3" else 14)
    else:
        mant, ex = np.frexp(amax / 6.0)
        byte = np.where(mant > 0.5, ex, ex - 1) + 127
    byte = np.clip(np.where(amax > 0, byte, 1), 1, 254)
    scaled = (w * np.exp2(127.0 - byte)[:, None, :]).reshape(k, n).astype(np.float32)
    by_word = np.ascontiguousarray(scaled.reshape(k // 512, 128, 4, n).transpose(0, 1, 3, 2))
    if fmt in ("e4m3", "e5m2"):
        words = by_word.astype(ml_dtypes.float8_e4m3fn if fmt == "e4m3" else ml_dtypes.float8_e5m2).view(np.uint8)
    else:
        c = by_word.astype(ml_dtypes.float4_e2m1fn).view(np.uint8) & 0xF
        words = (c[..., 0::2] | (c[..., 1::2] << 4)).reshape(k // 512, 128, 2 * n)
    return np.ascontiguousarray(words), np.ascontiguousarray(byte.astype(np.uint8).reshape(k // 512, 16, n))


def unpack_weight(words, scales, fmt):
    g, _, n = scales.shape
    words = np.ascontiguousarray(words).reshape(g, 128, n, -1)
    if fmt in ("e4m3", "e5m2"):
        vals = words.view(ml_dtypes.float8_e4m3fn if fmt == "e4m3" else ml_dtypes.float8_e5m2).astype(np.float64)
    else:
        nib = np.empty((g, 128, n, 4), np.uint8)
        nib[..., 0::2] = words & 0xF
        nib[..., 1::2] = words >> 4
        vals = E2M1[nib]
    vals = vals * np.repeat(np.exp2(scales.astype(np.float64) - 127.0), 8, axis=1)[..., None]
    return vals.transpose(0, 1, 3, 2).reshape(g * 512, n)


def sigmoid(v):
    return 1.0 / (1.0 + np.exp(-v))


K, T, J, R, N, E = 512, 2048, 256, 512, 256, 1024


def setup_inputs():
    n = np.random.standard_normal
    idx = np.random.permutation(T)[:J]
    idx2 = np.random.permutation(T)[:J]
    idx3 = np.random.permutation(E)[:J]
    fk = mx_kscale(K)
    fr = mx_kscale(R)
    xtp = pack_weight(n((K, T)) / fk[:, None], "e5m2")
    wp = pack_weight(n((K, R)) * 1 / np.sqrt(K) * fk[:, None] * fr, "e2m1")
    wbp = pack_weight(n((R, N)) * 1 / np.sqrt(R) / fr[:, None], "e2m1")
    wsp = pack_weight(n((K, N)) * 1 / np.sqrt(K) * fk[:, None], "e2m1")
    return {
        "xt_words": xtp[0],
        "xt_scales": xtp[1],
        "w_words": wp[0],
        "w_scales": wp[1],
        "wb_words": wbp[0],
        "wb_scales": wbp[1],
        "ws_words": wsp[0],
        "ws_scales": wsp[1],
        "tz": (n((N, E))).astype(np.float32),
        "so": (np.random.uniform(0.6, 1.6, (N, 1))).astype(np.float32),
        "bo": (np.random.uniform(-1.0, 1.0, (N, 1))).astype(np.float32),
        "offs": striped(idx),
        "offs2": striped(idx2),
        "offs3": striped(idx3),
    }


def reference(xt_words, xt_scales, w_words, w_scales, wb_words, wb_scales, ws_words, ws_scales, tz, so, bo, offs, offs2, offs3):
    idx = unstriped(offs)
    idx2 = unstriped(offs2)
    idx3 = unstriped(offs3)
    xtu = unpack_weight(xt_words, xt_scales, "e5m2")
    wu = unpack_weight(w_words, w_scales, "e2m1")
    wbu = unpack_weight(wb_words, wb_scales, "e2m1")
    wsu = unpack_weight(ws_words, ws_scales, "e2m1")
    xtidxg = xtu[:, idx]
    a = wu.T @ xtidxg
    xtidx2g = xtu[:, idx2]
    b = wu.T @ xtidx2g
    hid = np.abs(a - b)
    hidq = mxq(hid, 0, "e4m3")
    p = wbu.T @ hidq + wsu.T @ xtidx2g
    y = p * sigmoid(f64(tz)[:, idx3] * f64(so) + f64(bo))
    return y

@@ -1,0 +1,178 @@
+from contextlib import ExitStack
+
+import concourse.mybir as mybir
+
+K, T, J, R, N, E = 512, 2048, 256, 512, 256, 1024
+FLOPS = 2 * (2 * K * R * J + R * N * J + K * N * J)
+
+F32 = mybir.dt.float32
+BF16 = mybir.dt.bfloat16
+I32 = mybir.dt.int32
+U32 = mybir.dt.uint32
+U16 = mybir.dt.uint16
+U8 = mybir.dt.uint8
+E4M3X4 = mybir.dt.float8_e4m3fn_x4
+E5M2X4 = mybir.dt.float8_e5m2_x4
+E2M1X4 = mybir.dt.float4_e2m1fn_x4
+ACT = mybir.ActivationFunctionType
+ALU = mybir.AluOpType
+
+P = 128
+PACK = 4
+CHUNK = 128
+CHUNKS = J // CHUNK
+HALVES = N // P
+LIST_COLS = CHUNK // 16
+
+
+def load_scale_rows(queues, plane, scales):
+    rows = scales[0].bitcast(I32)
+    for q, queue in enumerate(queues):
+        queue.dma_start(out=plane.bitcast(I32)[32 * q : 32 * q + 4, :], in_=rows[4 * q : 4 * q + 4, :])
+
+
+def tile_list_tied_direct_skip_finalgate_kernel(
+    tc, xt_words, xt_scales, w_words, w_scales, wb_words, wb_scales, ws_words, ws_scales, tz, so, bo, offs, offs2, offs3, out
+):
+    nc = tc.nc
+    with ExitStack() as ctx:
+        sb = ctx.enter_context(tc.tile_pool(name="sb", bufs=1))
+        reuse = ctx.enter_context(tc.tile_pool(name="reuse", bufs=1))
+        ps = ctx.enter_context(tc.psum_pool(name="ps", bufs=1))
+
+        list1 = sb.tile([P, J // 16], U16, name="list1")
+        list2 = sb.tile([P, J // 16], U16, name="list2")
+        list3 = sb.tile([P, J // 16], U16, name="list3")
+        xt_w = sb.tile([P, T], U32, name="xt_w", align_bytes=64)
+        xt_s = reuse.tile([P, T], U8, name="xt_s", align_bytes=64, offset=8192)
+        w_raw = reuse.tile([P, 2 * R], U8, name="w_raw", align_bytes=64, offset=4096 - R)
+        w_raw_s = sb.tile([P, R], U8, name="w_raw_s", align_bytes=64)
+        w_w = sb.tile([P, 2 * R], U8, name="w_w", align_bytes=64)
+        w_s = sb.tile([P, R], U8, name="w_s", align_bytes=64)
+        wb_w = sb.tile([P, 2 * N], U8, name="wb_w", align_bytes=64)
+        ws_w = sb.tile([P, 2 * N], U8, name="ws_w", align_bytes=64)
+        late_s = reuse.tile([P, 2 * N], U8, name="late_s", align_bytes=64, offset=8192)
+        ws_s = late_s[:, :N]
+        wb_s = late_s[:, N:]
+        tz_rows = [reuse.tile([P, E], F32, name=f"tz{h}", align_bytes=64, offset=(8192 + 1024) * h) for h in range(HALVES)]
+        slope = reuse.tile([P, HALVES], F32, name="slope", align_bytes=64, offset=8192 + 512)
+        offset = reuse.tile([P, HALVES], F32, name="offset", align_bytes=64, offset=8192 + 576)
+
+        nc.vector.memset(xt_s[:].bitcast(I32), 0)
+        nc.vector.memset(w_raw_s[:].bitcast(I32), 0)
+
+        nc.sync.dma_start(list2[:], offs2)
+        nc.sync.dma_start(list1[:], offs)
+        nc.sync.dma_start(out=w_raw[:].bitcast(I32), in_=w_words[0].bitcast(I32))
+        load_scale_rows([nc.sync, nc.scalar] * 2, xt_s[:], xt_scales)
+        xt_rows = xt_words[0].rearrange("p c r -> p (c r)").bitcast(I32)
+        nc.sync.dma_start(out=xt_w[:].bitcast(I32)[:, :1280], in_=xt_rows[:, :1280])
+        load_scale_rows([nc.sync] * 4, w_raw_s[:], w_scales)
+        nc.sync.dma_start(out=xt_w[:].bitcast(I32)[:, 1280:], in_=xt_rows[:, 1280:])
+        nc.sync.dma_start(list3[:], offs3)
+        warm = sb.tile([P, 2], F32, name="warm")
+        nc.vector.memset(warm[:, 0:1], 0.0)
+        nc.scalar.activation(out=warm[:, 1:2], in_=warm[:, 0:1], func=ACT.Sigmoid)
+        nc.gpsimd.dma_start(out=ws_w[:].bitcast(I32), in_=ws_words[0].bitcast(I32))
+        nc.gpsimd.dma_start(out=wb_w[:].bitcast(I32), in_=wb_words[0].bitcast(I32))
+
+        nc.vector.tensor_copy(
+            out=w_w[:].bitcast(U16).rearrange("p (t m) -> p t m", t=PACK),
+            in_=w_raw[:].bitcast(U16).rearrange("p (m t) -> p t m", t=PACK),
+        )
+        x1_s = sb.tile([P, J], U8, name="x1_s", align_bytes=64)
+        x2_s = sb.tile([P, J], U8, name="x2_s", align_bytes=64)
+        nc.vector.tensor_copy(out=x2_s[:], in_=xt_s[:].indirect(list2[:]))
+        nc.vector.tensor_copy(out=x1_s[:], in_=xt_s[:].indirect(list1[:]))
+        nc.vector.tensor_copy(
+            out=w_s[:].rearrange("p (t m) -> p t m", t=PACK),
+            in_=w_raw_s[:].rearrange("p (m t) -> p t m", t=PACK),
+        )
+        nc.sync.dma_start(out=tz_rows[0][:], in_=tz[0:P, :])
+        with nc.allow_non_contiguous_dma(reason="one value a partition"):
+            nc.sync.dma_start(out=slope[:], in_=so.rearrange("(h p) o -> p (h o)", p=P))
+            nc.sync.dma_start(out=offset[:], in_=bo.rearrange("(h p) o -> p (h o)", p=P))
+        nc.sync.dma_start(out=tz_rows[1][:], in_=tz[P : 2 * P, :])
+        nc.vector.memset(late_s[:].bitcast(I32), 0)
+        load_scale_rows([nc.sync] * 4, ws_s, ws_scales)
+        load_scale_rows([nc.sync] * 3 + [nc.gpsimd], wb_s, wb_scales)
+
+        def first_product(name, token_list, scales):
+            words, banks = [], []
+            for c in range(CHUNKS):
+                picked = sb.tile([P, CHUNK], U32, name=f"x_{name}{c}", align_bytes=64)
+                nc.vector.tensor_copy(out=picked[:], in_=xt_w[:].indirect(token_list[:, c * LIST_COLS : (c + 1) * LIST_COLS]))
+                bank = ps.tile([P, PACK, CHUNK], F32, name=f"bank_{name}{c}")
+                for t in range(PACK):
+                    nc.tensor.matmul_mx(
+                        out=bank[:, t, :],
+                        lhsT=w_w[:, 2 * P * t : 2 * P * (t + 1)].bitcast(E2M1X4),
+                        lhsT_scale=w_s[:, P * t : P * (t + 1)],
+                        rhs=picked[:].bitcast(E5M2X4),
+                        rhs_scale=scales[:, c * CHUNK : (c + 1) * CHUNK],
+                        start=True,
+                        stop=True,
+                    )
+                words.append(picked)
+                banks.append(bank)
+            return words, banks
+
+        x2_w, bank_b = first_product("b", list2, x2_s)
+        x1_w, bank_a = first_product("a", list1, x1_s)
+
+        gates = [sb.tile([P, J], F32, name=f"gate{h}") for h in range(HALVES)]
+
+        def make_gate(h):
+            nc.scalar.activation(
+                out=gates[h][:],
+                in_=tz_rows[h][:].indirect(list3[:]),
+                func=ACT.Sigmoid,
+                bias=offset[:, h : h + 1],
+                scale=slope[:, h : h + 1],
+            )
+
+        b_sb = [sb.tile([P, CHUNK, PACK], F32, name=f"b_sb{c}") for c in range(CHUNKS)]
+        for c in range(CHUNKS):
+            nc.scalar.copy(out=b_sb[c][:], in_=bank_b[c][:].rearrange("p t j -> p j t"))
+        make_gate(0)
+        hid_bf = []
+        for c in range(CHUNKS):
+            diff = sb.tile([P, CHUNK, PACK], F32, name=f"diff{c}")
+            nc.vector.tensor_tensor(out=diff[:], in0=bank_a[c][:].rearrange("p t j -> p j t"), in1=b_sb[c][:], op=ALU.subtract)
+            hid = sb.tile([P, CHUNK * PACK], BF16, name=f"hid{c}", align_bytes=64)
+            nc.scalar.activation(out=hid[:], in_=diff[:].rearrange("p j t -> p (j t)"), func=ACT.Abs)
+            hid_bf.append(hid)
+        make_gate(1)
+
+        bank_p = [[ps.tile([P, CHUNK], F32, name=f"bank_p{c}{h}") for h in range(HALVES)] for c in range(CHUNKS)]
+        for c in range(CHUNKS):
+            for h in range(HALVES):
+                nc.tensor.matmul_mx(
+                    out=bank_p[c][h][:],
+                    lhsT=ws_w[:, 2 * P * h : 2 * P * (h + 1)].bitcast(E2M1X4),
+                    lhsT_scale=ws_s[:, P * h : P * (h + 1)],
+                    rhs=x2_w[c][:].bitcast(E5M2X4),
+                    rhs_scale=x2_s[:, c * CHUNK : (c + 1) * CHUNK],
+                    start=True,
+                    stop=False,
+                )
+        for c in range(CHUNKS):
+            hid_w = sb.tile([P, CHUNK], U32, name=f"hid_w{c}", align_bytes=64)
+            hid_s = sb.tile([P, CHUNK], U8, name=f"hid_s{c}", align_bytes=64)
+            nc.vector.quantize_mx(out=hid_w[:].bitcast(E4M3X4), scales=hid_s[:], in_=hid_bf[c][:])
+            for h in range(HALVES):
+                nc.tensor.matmul_mx(
+                    out=bank_p[c][h][:],
+                    lhsT=wb_w[:, 2 * P * h : 2 * P * (h + 1)].bitcast(E2M1X4),
+                    lhsT_scale=wb_s[:, P * h : P * (h + 1)],
+                    rhs=hid_w[:].bitcast(E4M3X4),
+                    rhs_scale=hid_s[:],
+                    start=False,
+                    stop=True,
+                )
+        for h, queue in enumerate((nc.scalar, nc.sync)):
+            result = sb.tile([P, J], F32, name=f"result{h}")
+            for c in range(CHUNKS):
+                slots = slice(c * CHUNK, (c + 1) * CHUNK)
+                nc.vector.tensor_tensor(out=result[:, slots], in0=bank_p[c][h][:], in1=gates[h][:, slots], op=ALU.mult)
+            queue.dma_start(out=out[h * P : (h + 1) * P, :], in_=result[:])

@@ -46,7 +46,7 @@ def tile_list_tied_direct_skip_finalgate_kernel(
         xt_w = sb.tile([P, T], U32, name="xt_w", align_bytes=64)
         xt_s = reuse.tile([P, T], U8, name="xt_s", align_bytes=64, offset=8192)
         w_raw = reuse.tile([P, 2 * R], U8, name="w_raw", align_bytes=64, offset=4096 - R)
-        w_raw_s = sb.tile([P, R], U8, name="w_raw_s", align_bytes=64)
+        w_raw_s = reuse.tile([P, R], U8, name="w_raw_s", align_bytes=64, offset=8192 + 2048)
         w_w = sb.tile([P, 2 * R], U8, name="w_w", align_bytes=64)
         w_s = sb.tile([P, R], U8, name="w_s", align_bytes=64)
         wb_w = sb.tile([P, 2 * N], U8, name="wb_w", align_bytes=64)
@@ -54,9 +54,9 @@ def tile_list_tied_direct_skip_finalgate_kernel(
         late_s = reuse.tile([P, 2 * N], U8, name="late_s", align_bytes=64, offset=8192)
         ws_s = late_s[:, :N]
         wb_s = late_s[:, N:]
-        tz_rows = [reuse.tile([P, E], F32, name=f"tz{h}", align_bytes=64, offset=(8192 + 1024) * h) for h in range(HALVES)]
-        slope = reuse.tile([P, HALVES], F32, name="slope", align_bytes=64, offset=8192 + 512)
-        offset = reuse.tile([P, HALVES], F32, name="offset", align_bytes=64, offset=8192 + 576)
+        tz_rows = [reuse.tile([P, E], F32, name=f"tz{h}", align_bytes=64, offset=(8192 + 2048) * h) for h in range(HALVES)]
+        slope = sb.tile([P, HALVES], F32, name="slope")
+        offset = sb.tile([P, HALVES], F32, name="offset")
 
         nc.vector.memset(xt_s[:].bitcast(I32), 0)
         nc.vector.memset(w_raw_s[:].bitcast(I32), 0)
@@ -66,13 +66,16 @@ def tile_list_tied_direct_skip_finalgate_kernel(
         nc.sync.dma_start(out=w_raw[:].bitcast(I32), in_=w_words[0].bitcast(I32))
         load_scale_rows([nc.sync, nc.scalar] * 2, xt_s[:], xt_scales)
         xt_rows = xt_words[0].rearrange("p c r -> p (c r)").bitcast(I32)
-        nc.sync.dma_start(out=xt_w[:].bitcast(I32)[:, :1280], in_=xt_rows[:, :1280])
+        nc.sync.dma_start(out=xt_w[:].bitcast(I32)[:, :1664], in_=xt_rows[:, :1664])
         load_scale_rows([nc.sync] * 4, w_raw_s[:], w_scales)
-        nc.sync.dma_start(out=xt_w[:].bitcast(I32)[:, 1280:], in_=xt_rows[:, 1280:])
+        nc.sync.dma_start(out=xt_w[:].bitcast(I32)[:, 1664:], in_=xt_rows[:, 1664:])
         nc.sync.dma_start(list3[:], offs3)
         warm = sb.tile([P, 2], F32, name="warm")
         nc.vector.memset(warm[:, 0:1], 0.0)
         nc.scalar.activation(out=warm[:, 1:2], in_=warm[:, 0:1], func=ACT.Sigmoid)
+        with nc.allow_non_contiguous_dma(reason="one value a partition"):
+            nc.gpsimd.dma_start(out=slope[:], in_=so.rearrange("(h p) o -> p (h o)", p=P))
+            nc.gpsimd.dma_start(out=offset[:], in_=bo.rearrange("(h p) o -> p (h o)", p=P))
         nc.gpsimd.dma_start(out=ws_w[:].bitcast(I32), in_=ws_words[0].bitcast(I32))
         nc.gpsimd.dma_start(out=wb_w[:].bitcast(I32), in_=wb_words[0].bitcast(I32))
 
@@ -84,18 +87,15 @@ def tile_list_tied_direct_skip_finalgate_kernel(
         x2_s = sb.tile([P, J], U8, name="x2_s", align_bytes=64)
         nc.vector.tensor_copy(out=x2_s[:], in_=xt_s[:].indirect(list2[:]))
         nc.vector.tensor_copy(out=x1_s[:], in_=xt_s[:].indirect(list1[:]))
+        nc.vector.memset(late_s[:].bitcast(I32), 0)
         nc.vector.tensor_copy(
             out=w_s[:].rearrange("p (t m) -> p t m", t=PACK),
             in_=w_raw_s[:].rearrange("p (m t) -> p t m", t=PACK),
         )
         nc.sync.dma_start(out=tz_rows[0][:], in_=tz[0:P, :])
-        with nc.allow_non_contiguous_dma(reason="one value a partition"):
-            nc.sync.dma_start(out=slope[:], in_=so.rearrange("(h p) o -> p (h o)", p=P))
-            nc.sync.dma_start(out=offset[:], in_=bo.rearrange("(h p) o -> p (h o)", p=P))
-        nc.sync.dma_start(out=tz_rows[1][:], in_=tz[P : 2 * P, :])
-        nc.vector.memset(late_s[:].bitcast(I32), 0)
         load_scale_rows([nc.sync] * 4, ws_s, ws_scales)
-        load_scale_rows([nc.sync] * 3 + [nc.gpsimd], wb_s, wb_scales)
+        load_scale_rows([nc.sync] * 4, wb_s, wb_scales)
+        nc.sync.dma_start(out=tz_rows[1][:], in_=tz[P : 2 * P, :])
 
         def first_product(name, token_list, scales):
             words, banks = [], []
@@ -132,15 +132,21 @@ def tile_list_tied_direct_skip_finalgate_kernel(
             )
 
         b_sb = [sb.tile([P, CHUNK, PACK], F32, name=f"b_sb{c}") for c in range(CHUNKS)]
-        for c in range(CHUNKS):
-            nc.scalar.copy(out=b_sb[c][:], in_=bank_b[c][:].rearrange("p t j -> p j t"))
+        nc.scalar.copy(out=b_sb[0][:], in_=bank_b[0][:].rearrange("p t j -> p j t"))
+        nc.vector.tensor_copy(out=b_sb[1][:], in_=bank_b[1][:].rearrange("p t j -> p j t"))
         make_gate(0)
         hid_bf = []
         for c in range(CHUNKS):
-            diff = sb.tile([P, CHUNK, PACK], F32, name=f"diff{c}")
-            nc.vector.tensor_tensor(out=diff[:], in0=bank_a[c][:].rearrange("p t j -> p j t"), in1=b_sb[c][:], op=ALU.subtract)
-            hid = sb.tile([P, CHUNK * PACK], BF16, name=f"hid{c}", align_bytes=64)
-            nc.scalar.activation(out=hid[:], in_=diff[:].rearrange("p j t -> p (j t)"), func=ACT.Abs)
+            hid = reuse.tile([P, CHUNK, PACK], BF16, name=f"hid{c}", align_bytes=64, offset=1024 * c)
+            pieces = 2
+            width = CHUNK // pieces
+            for i in range(pieces):
+                slots = slice(i * width, (i + 1) * width)
+                diff = sb.tile([P, width, PACK], F32, name=f"diff{c}{i}")
+                nc.vector.tensor_tensor(
+                    out=diff[:], in0=bank_a[c][:, :, slots].rearrange("p t j -> p j t"), in1=b_sb[c][:, slots, :], op=ALU.subtract
+                )
+                nc.scalar.activation(out=hid[:, slots, :], in_=diff[:], func=ACT.Abs)
             hid_bf.append(hid)
         make_gate(1)
 
@@ -159,7 +165,7 @@ def tile_list_tied_direct_skip_finalgate_kernel(
         for c in range(CHUNKS):
             hid_w = sb.tile([P, CHUNK], U32, name=f"hid_w{c}", align_bytes=64)
             hid_s = sb.tile([P, CHUNK], U8, name=f"hid_s{c}", align_bytes=64)
-            nc.vector.quantize_mx(out=hid_w[:].bitcast(E4M3X4), scales=hid_s[:], in_=hid_bf[c][:])
+            nc.vector.quantize_mx(out=hid_w[:].bitcast(E4M3X4), scales=hid_s[:], in_=hid_bf[c][:].rearrange("p j t -> p (j t)"))
             for h in range(HALVES):
                 nc.tensor.matmul_mx(
                     out=bank_p[c][h][:],
@@ -170,9 +176,9 @@ def tile_list_tied_direct_skip_finalgate_kernel(
                     start=False,
                     stop=True,
                 )
-        for h, queue in enumerate((nc.scalar, nc.sync)):
-            result = sb.tile([P, J], F32, name=f"result{h}")
-            for c in range(CHUNKS):
+        for h in range(HALVES):
+            for c, queue in enumerate((nc.scalar if h else nc.sync, nc.sync)):
                 slots = slice(c * CHUNK, (c + 1) * CHUNK)
-                nc.vector.tensor_tensor(out=result[:, slots], in0=bank_p[c][h][:], in1=gates[h][:, slots], op=ALU.mult)
-            queue.dma_start(out=out[h * P : (h + 1) * P, :], in_=result[:])
+                result = sb.tile([P, CHUNK], F32, name=f"result{c}{h}")
+                nc.vector.tensor_tensor(out=result[:], in0=bank_p[c][h][:], in1=gates[h][:, slots], op=ALU.mult)
+                queue.dma_start(out=out[h * P : (h + 1) * P, slots], in_=result[:])

@@ -46,15 +46,14 @@ def tile_list_tied_direct_skip_finalgate_kernel(
         xt_w = sb.tile([P, T], U32, name="xt_w", align_bytes=64)
         xt_s = reuse.tile([P, T], U8, name="xt_s", align_bytes=64, offset=8192)
         w_raw = reuse.tile([P, 2 * R], U8, name="w_raw", align_bytes=64, offset=4096 - R)
-        w_raw_s = reuse.tile([P, R], U8, name="w_raw_s", align_bytes=64, offset=8192 + 2048)
+        w_raw_s = sb.tile([P, R], U8, name="w_raw_s", align_bytes=64)
         w_w = sb.tile([P, 2 * R], U8, name="w_w", align_bytes=64)
         w_s = sb.tile([P, R], U8, name="w_s", align_bytes=64)
-        wb_w = sb.tile([P, 2 * N], U8, name="wb_w", align_bytes=64)
-        ws_w = sb.tile([P, 2 * N], U8, name="ws_w", align_bytes=64)
-        late_s = reuse.tile([P, 2 * N], U8, name="late_s", align_bytes=64, offset=8192)
-        ws_s = late_s[:, :N]
-        wb_s = late_s[:, N:]
-        tz_rows = [reuse.tile([P, E], F32, name=f"tz{h}", align_bytes=64, offset=(8192 + 2048) * h) for h in range(HALVES)]
+        wb_w = reuse.tile([P, 2 * N], U8, name="wb_w", align_bytes=64, offset=8192 + 1024)
+        ws_w = reuse.tile([P, 2 * N], U8, name="ws_w", align_bytes=64, offset=8192 + 512)
+        ws_s = reuse.tile([P, N], U8, name="ws_s", align_bytes=64, offset=8192)
+        wb_s = sb.tile([P, N], U8, name="wb_s", align_bytes=64)
+        tz_rows = [reuse.tile([P, E], F32, name=f"tz{h}", align_bytes=64, offset=4096 * h) for h in range(HALVES)]
         slope = sb.tile([P, HALVES], F32, name="slope")
         offset = sb.tile([P, HALVES], F32, name="offset")
 
@@ -73,11 +72,11 @@ def tile_list_tied_direct_skip_finalgate_kernel(
         warm = sb.tile([P, 2], F32, name="warm")
         nc.vector.memset(warm[:, 0:1], 0.0)
         nc.scalar.activation(out=warm[:, 1:2], in_=warm[:, 0:1], func=ACT.Sigmoid)
+        nc.vector.memset(wb_s[:].bitcast(I32), 0)
         with nc.allow_non_contiguous_dma(reason="one value a partition"):
             nc.gpsimd.dma_start(out=slope[:], in_=so.rearrange("(h p) o -> p (h o)", p=P))
             nc.gpsimd.dma_start(out=offset[:], in_=bo.rearrange("(h p) o -> p (h o)", p=P))
-        nc.gpsimd.dma_start(out=ws_w[:].bitcast(I32), in_=ws_words[0].bitcast(I32))
-        nc.gpsimd.dma_start(out=wb_w[:].bitcast(I32), in_=wb_words[0].bitcast(I32))
+        load_scale_rows([nc.gpsimd] * 4, wb_s[:], wb_scales)
 
         nc.vector.tensor_copy(
             out=w_w[:].bitcast(U16).rearrange("p (t m) -> p t m", t=PACK),
@@ -87,15 +86,16 @@ def tile_list_tied_direct_skip_finalgate_kernel(
         x2_s = sb.tile([P, J], U8, name="x2_s", align_bytes=64)
         nc.vector.tensor_copy(out=x2_s[:], in_=xt_s[:].indirect(list2[:]))
         nc.vector.tensor_copy(out=x1_s[:], in_=xt_s[:].indirect(list1[:]))
-        nc.vector.memset(late_s[:].bitcast(I32), 0)
+        nc.vector.memset(ws_s[:].bitcast(I32), 0)
         nc.vector.tensor_copy(
             out=w_s[:].rearrange("p (t m) -> p t m", t=PACK),
             in_=w_raw_s[:].rearrange("p (m t) -> p t m", t=PACK),
         )
-        nc.sync.dma_start(out=tz_rows[0][:], in_=tz[0:P, :])
-        load_scale_rows([nc.sync] * 4, ws_s, ws_scales)
-        load_scale_rows([nc.sync] * 4, wb_s, wb_scales)
-        nc.sync.dma_start(out=tz_rows[1][:], in_=tz[P : 2 * P, :])
+        for h in range(HALVES):
+            nc.sync.dma_start(out=tz_rows[h][:], in_=tz[h * P : (h + 1) * P, :])
+        nc.sync.dma_start(out=ws_w[:].bitcast(I32), in_=ws_words[0].bitcast(I32))
+        nc.sync.dma_start(out=wb_w[:].bitcast(I32), in_=wb_words[0].bitcast(I32))
+        load_scale_rows([nc.sync] * 4, ws_s[:], ws_scales)
 
         def first_product(name, token_list, scales):
             words, banks = [], []

from contextlib import ExitStack

import concourse.mybir as mybir

K, T, J, R, N, E = 512, 2048, 256, 512, 256, 1024
FLOPS = 2 * (2 * K * R * J + R * N * J + K * N * J)

F32 = mybir.dt.float32
BF16 = mybir.dt.bfloat16
I32 = mybir.dt.int32
U32 = mybir.dt.uint32
U16 = mybir.dt.uint16
U8 = mybir.dt.uint8
E4M3X4 = mybir.dt.float8_e4m3fn_x4
E5M2X4 = mybir.dt.float8_e5m2_x4
E2M1X4 = mybir.dt.float4_e2m1fn_x4
ACT = mybir.ActivationFunctionType
ALU = mybir.AluOpType

P = 128
PACK = 4
CHUNK = 128
CHUNKS = J // CHUNK
HALVES = N // P
LIST_COLS = CHUNK // 16


def load_scale_rows(queues, plane, scales):
    rows = scales[0].bitcast(I32)
    for q, queue in enumerate(queues):
        queue.dma_start(out=plane.bitcast(I32)[32 * q : 32 * q + 4, :], in_=rows[4 * q : 4 * q + 4, :])


def tile_list_tied_direct_skip_finalgate_kernel(
    tc, xt_words, xt_scales, w_words, w_scales, wb_words, wb_scales, ws_words, ws_scales, tz, so, bo, offs, offs2, offs3, out
):
    nc = tc.nc
    with ExitStack() as ctx:
        sb = ctx.enter_context(tc.tile_pool(name="sb", bufs=1))
        reuse = ctx.enter_context(tc.tile_pool(name="reuse", bufs=1))
        ps = ctx.enter_context(tc.psum_pool(name="ps", bufs=1))

        list1 = sb.tile([P, J // 16], U16, name="list1")
        list2 = sb.tile([P, J // 16], U16, name="list2")
        list3 = sb.tile([P, J // 16], U16, name="list3")
        xt_w = sb.tile([P, T], U32, name="xt_w", align_bytes=64)
        xt_s = reuse.tile([P, T], U8, name="xt_s", align_bytes=64, offset=8192)
        w_raw = reuse.tile([P, 2 * R], U8, name="w_raw", align_bytes=64, offset=4096 - R)
        w_raw_s = sb.tile([P, R], U8, name="w_raw_s", align_bytes=64)
        w_w = sb.tile([P, 2 * R], U8, name="w_w", align_bytes=64)
        w_s = sb.tile([P, R], U8, name="w_s", align_bytes=64)
        wb_w = reuse.tile([P, 2 * N], U8, name="wb_w", align_bytes=64, offset=8192 + 1024)
        ws_w = reuse.tile([P, 2 * N], U8, name="ws_w", align_bytes=64, offset=8192 + 512)
        ws_s = reuse.tile([P, N], U8, name="ws_s", align_bytes=64, offset=8192)
        wb_s = sb.tile([P, N], U8, name="wb_s", align_bytes=64)
        tz_rows = [reuse.tile([P, E], F32, name=f"tz{h}", align_bytes=64, offset=4096 * h) for h in range(HALVES)]
        slope = sb.tile([P, HALVES], F32, name="slope")
        offset = sb.tile([P, HALVES], F32, name="offset")

        nc.vector.memset(xt_s[:].bitcast(I32), 0)
        nc.vector.memset(w_raw_s[:].bitcast(I32), 0)

        nc.sync.dma_start(list2[:], offs2)
        nc.sync.dma_start(list1[:], offs)
        nc.sync.dma_start(out=w_raw[:].bitcast(I32), in_=w_words[0].bitcast(I32))
        load_scale_rows([nc.sync, nc.scalar] * 2, xt_s[:], xt_scales)
        xt_rows = xt_words[0].rearrange("p c r -> p (c r)").bitcast(I32)
        nc.sync.dma_start(out=xt_w[:].bitcast(I32)[:, :1664], in_=xt_rows[:, :1664])
        load_scale_rows([nc.sync] * 4, w_raw_s[:], w_scales)
        nc.sync.dma_start(out=xt_w[:].bitcast(I32)[:, 1664:], in_=xt_rows[:, 1664:])
        nc.sync.dma_start(list3[:], offs3)
        warm = sb.tile([P, 2], F32, name="warm")
        nc.vector.memset(warm[:, 0:1], 0.0)
        nc.scalar.activation(out=warm[:, 1:2], in_=warm[:, 0:1], func=ACT.Sigmoid)
        nc.vector.memset(wb_s[:].bitcast(I32), 0)
        with nc.allow_non_contiguous_dma(reason="one value a partition"):
            nc.gpsimd.dma_start(out=slope[:], in_=so.rearrange("(h p) o -> p (h o)", p=P))
            nc.gpsimd.dma_start(out=offset[:], in_=bo.rearrange("(h p) o -> p (h o)", p=P))
        load_scale_rows([nc.gpsimd] * 4, wb_s[:], wb_scales)

        nc.vector.tensor_copy(
            out=w_w[:].bitcast(U16).rearrange("p (t m) -> p t m", t=PACK),
            in_=w_raw[:].bitcast(U16).rearrange("p (m t) -> p t m", t=PACK),
        )
        x1_s = sb.tile([P, J], U8, name="x1_s", align_bytes=64)
        x2_s = sb.tile([P, J], U8, name="x2_s", align_bytes=64)
        nc.vector.tensor_copy(out=x2_s[:], in_=xt_s[:].indirect(list2[:]))
        nc.vector.tensor_copy(out=x1_s[:], in_=xt_s[:].indirect(list1[:]))
        nc.vector.memset(ws_s[:].bitcast(I32), 0)
        nc.vector.tensor_copy(
            out=w_s[:].rearrange("p (t m) -> p t m", t=PACK),
            in_=w_raw_s[:].rearrange("p (m t) -> p t m", t=PACK),
        )
        for h in range(HALVES):
            nc.sync.dma_start(out=tz_rows[h][:], in_=tz[h * P : (h + 1) * P, :])
        nc.sync.dma_start(out=ws_w[:].bitcast(I32), in_=ws_words[0].bitcast(I32))
        nc.sync.dma_start(out=wb_w[:].bitcast(I32), in_=wb_words[0].bitcast(I32))
        load_scale_rows([nc.sync] * 4, ws_s[:], ws_scales)

        def first_product(name, token_list, scales):
            words, banks = [], []
            for c in range(CHUNKS):
                picked = sb.tile([P, CHUNK], U32, name=f"x_{name}{c}", align_bytes=64)
                nc.vector.tensor_copy(out=picked[:], in_=xt_w[:].indirect(token_list[:, c * LIST_COLS : (c + 1) * LIST_COLS]))
                bank = ps.tile([P, PACK, CHUNK], F32, name=f"bank_{name}{c}")
                for t in range(PACK):
                    nc.tensor.matmul_mx(
                        out=bank[:, t, :],
                        lhsT=w_w[:, 2 * P * t : 2 * P * (t + 1)].bitcast(E2M1X4),
                        lhsT_scale=w_s[:, P * t : P * (t + 1)],
                        rhs=picked[:].bitcast(E5M2X4),
                        rhs_scale=scales[:, c * CHUNK : (c + 1) * CHUNK],
                        start=True,
                        stop=True,
                    )
                words.append(picked)
                banks.append(bank)
            return words, banks

        x2_w, bank_b = first_product("b", list2, x2_s)
        x1_w, bank_a = first_product("a", list1, x1_s)

        gates = [sb.tile([P, J], F32, name=f"gate{h}") for h in range(HALVES)]

        def make_gate(h):
            nc.scalar.activation(
                out=gates[h][:],
                in_=tz_rows[h][:].indirect(list3[:]),
                func=ACT.Sigmoid,
                bias=offset[:, h : h + 1],
                scale=slope[:, h : h + 1],
            )

        b_sb = [sb.tile([P, CHUNK, PACK], F32, name=f"b_sb{c}") for c in range(CHUNKS)]
        nc.scalar.copy(out=b_sb[0][:], in_=bank_b[0][:].rearrange("p t j -> p j t"))
        nc.vector.tensor_copy(out=b_sb[1][:], in_=bank_b[1][:].rearrange("p t j -> p j t"))
        make_gate(0)
        hid_bf = []
        for c in range(CHUNKS):
            hid = reuse.tile([P, CHUNK, PACK], BF16, name=f"hid{c}", align_bytes=64, offset=1024 * c)
            pieces = 2
            width = CHUNK // pieces
            for i in range(pieces):
                slots = slice(i * width, (i + 1) * width)
                diff = sb.tile([P, width, PACK], F32, name=f"diff{c}{i}")
                nc.vector.tensor_tensor(
                    out=diff[:], in0=bank_a[c][:, :, slots].rearrange("p t j -> p j t"), in1=b_sb[c][:, slots, :], op=ALU.subtract
                )
                nc.scalar.activation(out=hid[:, slots, :], in_=diff[:], func=ACT.Abs)
            hid_bf.append(hid)
        make_gate(1)

        bank_p = [[ps.tile([P, CHUNK], F32, name=f"bank_p{c}{h}") for h in range(HALVES)] for c in range(CHUNKS)]
        for c in range(CHUNKS):
            for h in range(HALVES):
                nc.tensor.matmul_mx(
                    out=bank_p[c][h][:],
                    lhsT=ws_w[:, 2 * P * h : 2 * P * (h + 1)].bitcast(E2M1X4),
                    lhsT_scale=ws_s[:, P * h : P * (h + 1)],
                    rhs=x2_w[c][:].bitcast(E5M2X4),
                    rhs_scale=x2_s[:, c * CHUNK : (c + 1) * CHUNK],
                    start=True,
                    stop=False,
                )
        for c in range(CHUNKS):
            hid_w = sb.tile([P, CHUNK], U32, name=f"hid_w{c}", align_bytes=64)
            hid_s = sb.tile([P, CHUNK], U8, name=f"hid_s{c}", align_bytes=64)
            nc.vector.quantize_mx(out=hid_w[:].bitcast(E4M3X4), scales=hid_s[:], in_=hid_bf[c][:].rearrange("p j t -> p (j t)"))
            for h in range(HALVES):
                nc.tensor.matmul_mx(
                    out=bank_p[c][h][:],
                    lhsT=wb_w[:, 2 * P * h : 2 * P * (h + 1)].bitcast(E2M1X4),
                    lhsT_scale=wb_s[:, P * h : P * (h + 1)],
                    rhs=hid_w[:].bitcast(E4M3X4),
                    rhs_scale=hid_s[:],
                    start=False,
                    stop=True,
                )
        for h in range(HALVES):
            for c, queue in enumerate((nc.scalar if h else nc.sync, nc.sync)):
                slots = slice(c * CHUNK, (c + 1) * CHUNK)
                result = sb.tile([P, CHUNK], F32, name=f"result{c}{h}")
                nc.vector.tensor_tensor(out=result[:], in0=bank_p[c][h][:], in1=gates[h][:, slots], op=ALU.mult)
                queue.dma_start(out=out[h * P : (h + 1) * P, slots], in_=result[:])
